import numpy as np
import ml_dtypes


def mxq(x, axis, fmt="e4m3"):
    dtype, down = {"e4m3": (ml_dtypes.float8_e4m3fn, 7), "e5m2": (ml_dtypes.float8_e5m2, 14)}[fmt]
    v = np.moveaxis(np.asarray(x, np.float32).astype(ml_dtypes.bfloat16).astype(np.float64), axis, -1)
    blocks = v.reshape(v.shape[:-1] + (-1, 32))
    amax = np.abs(blocks).max(-1, keepdims=True)
    byte = np.maximum(np.where(amax > 0, np.frexp(amax)[1] - 1 + 127, 0) - down, 1)
    scale = np.exp2(byte - 127.0)
    codes = (blocks / scale).astype(np.float32).astype(dtype).astype(np.float64)
    return np.moveaxis((codes * scale).reshape(v.shape), -1, axis)


WIDE = False


def mx_kscale(k):
    if not WIDE:
        return np.ones(k)
    levels = np.array([30, -30])
    if k % 512:
        return np.exp2(np.random.permutation(np.resize(levels, k // 32))).repeat(32)
    a = np.empty((k // 512, 16))
    for p in range(k // 512):
        a[p, :8] = np.random.permutation(np.resize(levels, 8))
        for g in range(8):
            far = levels[np.abs(levels - a[p, g]) >= 10]
            a[p, g + 8] = far[np.random.randint(len(far))]
    return np.exp2(a.ravel()).repeat(32)


def f64(x):
    return np.asarray(x).astype(np.float64)


def striped(idx):
    return np.tile(np.asarray(idx).reshape(-1, 16).T, (8, 1)).astype(np.uint16)


def unstriped(offs):
    return offs[:16].T.reshape(-1).astype(np.int64)


def striped8(idx):
    return np.asarray(idx).reshape(8, -1, 16).transpose(0, 2, 1).reshape(128, -1).astype(np.uint16)


def unstriped8(offs):
    return offs.reshape(8, 16, -1).transpose(0, 2, 1).reshape(8, -1).astype(np.int64)


def pick8(x, idx, run):
    r = np.arange(len(x))
    return x[r[:, None], idx[r % (8 * run) // run]]


E2M1 = np.array([0.0, 0.5, 1.0, 1.5, 2.0, 3.0, 4.0, 6.0, -0.0, -0.5, -1.0, -1.5, -2.0, -3.0, -4.0, -6.0])


def pack_weight(w, fmt):
    k, n = w.shape
    w = f64(np.asarray(w, np.float32).astype(ml_dtypes.bfloat16)).reshape(k // 32, 32, n)
    amax = np.abs(w).max(1)
    if fmt == "e4m3":
        byte = np.frexp(amax)[1] - 1 + 127 - 7
    else:
        mant, ex = np.frexp(amax / 6.0)
        byte = np.where(mant > 0.5, ex, ex - 1) + 127
    byte = np.clip(np.where(amax > 0, byte, 1), 1, 254)
    scaled = (w * np.exp2(127.0 - byte)[:, None, :]).reshape(k, n).astype(np.float32)
    by_word = np.ascontiguousarray(scaled.reshape(k // 512, 128, 4, n).transpose(0, 1, 3, 2))
    if fmt == "e4m3":
        words = by_word.astype(ml_dtypes.float8_e4m3fn).view(np.uint8)
    else:
        c = by_word.astype(ml_dtypes.float4_e2m1fn).view(np.uint8) & 0xF
        words = (c[..., 0::2] | (c[..., 1::2] << 4)).reshape(k // 512, 128, 2 * n)
    return np.ascontiguousarray(words), np.ascontiguousarray(byte.astype(np.uint8).reshape(k // 512, 16, n))


def unpack_weight(words, scales, fmt):
    g, _, n = scales.shape
    words = np.ascontiguousarray(words).reshape(g, 128, n, -1)
    if fmt == "e4m3":
        vals = words.view(ml_dtypes.float8_e4m3fn).astype(np.float64)
    else:
        nib = np.empty((g, 128, n, 4), np.uint8)
        nib[..., 0::2] = words & 0xF
        nib[..., 1::2] = words >> 4
        vals = E2M1[nib]
    vals = vals * np.repeat(np.exp2(scales.astype(np.float64) - 127.0), 8, axis=1)[..., None]
    return vals.transpose(0, 1, 3, 2).reshape(g * 512, n)


def sigmoid(v):
    return 1.0 / (1.0 + np.exp(-v))


def sgn(shape):
    return np.random.uniform(0.5, 2.0, shape) * np.where(np.random.standard_normal(shape) < 0, -1.0, 1.0)


K, T, J, R, V, C, O, N, E = 512, 1024, 256, 512, 1024, 512, 256, 256, 512


def setup_inputs():
    n = np.random.standard_normal
    idx = np.random.permutation(V)[:R]
    idx2 = np.random.permutation(T)[:J]
    idx3 = np.stack([np.random.permutation(C)[:J] for _ in range(8)])
    idx4 = np.stack([np.random.permutation(C)[:O] for _ in range(8)])
    idx5 = np.stack([np.random.permutation(C)[:O] for _ in range(8)])
    idx6 = np.random.permutation(E)[:O]
    idx7 = np.random.permutation(E)[:O]
    fk = mx_kscale(K)
    fr = mx_kscale(R)
    xtp = pack_weight(n((K, T)) / fk[:, None], "e2m1")
    wtp = pack_weight(n((K, V)) * 1 / np.sqrt(K) * fk[:, None], "e4m3")
    wbp = pack_weight(n((R, N)) * 1 / np.sqrt(R) / fr[:, None], "e2m1")
    return {
        "xt_words": xtp[0],
        "xt_scales": xtp[1],
        "wt_words": wtp[0],
        "wt_scales": wtp[1],
        "sa": (np.random.uniform(0.5, 1.6, (R, 1)) * fr[:, None]).astype(np.float32),
        "sg": (sgn((R, 1))).astype(np.float32),
        "bg": (np.random.uniform(-2.0, 2.0, (R, 1))).astype(np.float32),
        "wb_words": wbp[0],
        "wb_scales": wbp[1],
        "offs": striped(idx),
        "offs2": striped(idx2),
        "offs3": striped8(idx3),
        "offs4": striped8(idx4),
        "offs5": striped8(idx5),
        "offs6": striped(idx6),
        "offs7": striped(idx7),
    }


def reference(xt_words, xt_scales, wt_words, wt_scales, sa, sg, bg, wb_words, wb_scales, offs, offs2, offs3, offs4, offs5, offs6, offs7):
    idx = unstriped(offs)
    idx2 = unstriped(offs2)
    idx3 = unstriped8(offs3)
    idx4 = unstriped8(offs4)
    idx5 = unstriped8(offs5)
    idx6 = unstriped(offs6)
    idx7 = unstriped(offs7)
    xtu = unpack_weight(xt_words, xt_scales, "e2m1")
    wtu = unpack_weight(wt_words, wt_scales, "e4m3")
    wbu = unpack_weight(wb_words, wb_scales, "e2m1")
    wtidxg = wtu[:, idx]
    xtidx2g = xtu[:, idx2]
    a = wtidxg.T @ xtidx2g
    pw = np.zeros((R, C))
    pw[np.arange(R)[:, None], idx3[np.arange(R) % 512 // 64]] = a
    hid = pick8(pw, idx4, 64) * f64(sa) * sigmoid(pick8(pw, idx5, 64) * f64(sg) + f64(bg))
    hidq = mxq(hid, 0, "e5m2")
    p = wbu.T @ hidq
    pa = np.zeros((N, E))
    pa[:, idx6] = p
    pb = np.zeros((N, E))
    pb[:, idx7] = p
    y = pa + pb
    return y

@@ -1,0 +1,173 @@
+from contextlib import ExitStack
+
+import concourse.mybir as mybir
+
+K, T, J, R, V, C, O, N, E = 512, 1024, 256, 512, 1024, 512, 256, 256, 512
+FLOPS = 2 * K * R * J + 2 * R * N * O
+
+F32 = mybir.dt.float32
+BF16 = mybir.dt.bfloat16
+I32 = mybir.dt.int32
+U32 = mybir.dt.uint32
+U16 = mybir.dt.uint16
+U8 = mybir.dt.uint8
+E4M3X4 = mybir.dt.float8_e4m3fn_x4
+E5M2X4 = mybir.dt.float8_e5m2_x4
+E2M1X4 = mybir.dt.float4_e2m1fn_x4
+ACT = mybir.ActivationFunctionType
+ALU = mybir.AluOpType
+
+P = 128
+PACK = 4
+HALF = O // 2
+
+
+def load_scales(queue, plane, scales):
+    for q in range(4):
+        queue.dma_start(out=plane[32 * q : 32 * q + 4, :].bitcast(I32), in_=scales[0, 4 * q : 4 * q + 4, :].bitcast(I32))
+
+
+def tile_list_gatedgroupboard_chosen_one_pagetwice_kernel(
+    tc, xt_words, xt_scales, wt_words, wt_scales, sa, sg, bg, wb_words, wb_scales,
+    offs, offs2, offs3, offs4, offs5, offs6, offs7, out,
+):
+    nc = tc.nc
+    with ExitStack() as ctx:
+        sb = ctx.enter_context(tc.tile_pool(name="sb", bufs=1))
+        late = ctx.enter_context(tc.tile_pool(name="late", bufs=1))
+        ps = ctx.enter_context(tc.psum_pool(name="ps", bufs=1))
+
+        def list_tile(name, src):
+            t = sb.tile([P, src.shape[1]], U16, name=name)
+            nc.sync.dma_start(t[:], src)
+            return t
+
+        xs = late.tile([P, T], U8, name="xs", align_bytes=64, offset=4 * E - T // 2)
+        ws = sb.tile([P, V], U8, name="ws", align_bytes=64)
+        bs = sb.tile([P, N], U8, name="bs", align_bytes=64)
+        nc.vector.memset(ws[:].bitcast(I32), 0)
+        nc.vector.memset(xs[:].bitcast(I32), 0)
+        nc.vector.memset(bs[:].bitcast(I32), 0)
+
+        l2 = list_tile("l2", offs2)
+        xw = sb.tile([P, T], U16, name="xw", align_bytes=64)
+        nc.sync.dma_start(out=xw[:].bitcast(I32), in_=xt_words[0].bitcast(I32))
+        l1 = list_tile("l1", offs)
+        load_scales(nc.sync, ws, wt_scales)
+        ww = sb.tile([P, V], U32, name="ww", align_bytes=64)
+        nc.sync.dma_start(out=ww[:].bitcast(I32), in_=wt_words[0].rearrange("p n t -> p (n t)").bitcast(I32))
+        load_scales(nc.sync, xs, xt_scales)
+        l3 = list_tile("l3", offs3)
+        l5 = list_tile("l5", offs5)
+
+        def row_values(name, src):
+            t = sb.tile([P, PACK], F32, name=name)
+            nc.sync.dma_start(out=t[:], in_=src.rearrange("(p t) one -> p (t one)", t=PACK))
+            return t
+
+        sg_t = row_values("sg_t", sg)
+        bg_t = row_values("bg_t", bg)
+        l4 = list_tile("l4", offs4)
+        sa_t = row_values("sa_t", sa)
+        bw = sb.tile([P, 2 * N], U8, name="bw", align_bytes=64)
+        nc.sync.dma_start(out=bw[:].bitcast(I32), in_=wb_words[0].bitcast(I32))
+        load_scales(nc.sync, bs, wb_scales)
+        l6 = list_tile("l6", offs6)
+        l7 = list_tile("l7", offs7)
+
+        board = [sb.tile([P, C], F32, name="board%d" % t) for t in range(PACK)]
+        pa = [sb.tile([P, E], F32, name="pa0")]
+        pb = [sb.tile([P, E], F32, name="pb0")]
+        for t in range(PACK):
+            nc.vector.memset(board[t][:], 0.0)
+        nc.vector.memset(pa[0][:], 0.0)
+        nc.vector.memset(pb[0][:], 0.0)
+
+        xg = sb.tile([P, J], U16, name="xg", align_bytes=64)
+        xgs = sb.tile([P, J], U8, name="xgs", align_bytes=64)
+        wg = sb.tile([P, PACK, P], U32, name="wg", align_bytes=64)
+        wgs = sb.tile([P, PACK, P], U8, name="wgs", align_bytes=64)
+        nc.vector.tensor_copy(xg[:], xw[:].indirect(l2[:]))
+        nc.vector.tensor_copy(wgs[:].rearrange("p t q -> p q t"), ws[:].indirect(l1[:]))
+        nc.vector.tensor_copy(wg[:].rearrange("p t q -> p q t"), ww[:].indirect(l1[:]))
+        halves = [(slice(h * HALF, (h + 1) * HALF), slice(h * HALF // 16, (h + 1) * HALF // 16)) for h in range(2)]
+        whole = [(slice(0, O), slice(0, O // 16))]
+        for cols, lcols in halves:
+            nc.vector.tensor_copy(xgs[:, cols], xs[:].indirect(l2[:, lcols]))
+        pa.append(late.tile([P, E], F32, name="pa1", offset=0))
+        pb.append(late.tile([P, E], F32, name="pb1", offset=4 * E))
+        nc.vector.memset(pa[1][:], 0.0)
+        nc.vector.memset(pb[1][:], 0.0)
+
+        a_sb = {}
+        for t in range(PACK):
+            for i, (cols, lcols) in enumerate(halves if t == 0 else whole):
+                w = cols.stop - cols.start
+                acc = ps.tile([P, w], F32, name="acc%d%d" % (t, i), tag="bank%d" % (len(a_sb)))
+                nc.tensor.matmul_mx(out=acc[:], lhsT=wg[:, t, :].bitcast(E4M3X4), lhsT_scale=wgs[:, t, :],
+                                    rhs=xg[:, cols].bitcast(E2M1X4), rhs_scale=xgs[:, cols], start=True, stop=True)
+                a_t = sb.tile([P, w], F32, name="a%d%d" % (t, i))
+                nc.scalar.copy(a_t[:], acc[:])
+                a_sb[t, i] = a_t
+
+        val = [sb.tile([P, 2, O], F32, name="val%d" % u) for u in range(2)]
+        gate = [sb.tile([P, 2, O], F32, name="gate%d" % u) for u in range(2)]
+        hid = [sb.tile([P, HALF, PACK], BF16, name="hid%d" % h, align_bytes=64) for h in range(2)]
+
+        def fetch(t, cols, lcols):
+            u, e = divmod(t, 2)
+            nc.scalar.activation(out=gate[u][:, e, cols], in_=board[t][:].indirect(l5[:, lcols]), func=ACT.Sigmoid,
+                                 bias=bg_t[:, t : t + 1], scale=sg_t[:, t : t + 1])
+            nc.scalar.activation(out=val[u][:, e, cols], in_=board[t][:].indirect(l4[:, lcols]), func=ACT.Copy,
+                                 scale=sa_t[:, t : t + 1])
+
+        for t in range(PACK):
+            for i, (cols, lcols) in enumerate(halves if t == 0 else whole):
+                nc.vector.tensor_copy(board[t][:].indirect(l3[:, lcols]), a_sb[t, i][:])
+            for cols, lcols in halves if t == PACK - 1 else whole:
+                fetch(t, cols, lcols)
+
+        def gate_pair(u, h):
+            cols = halves[h][0]
+            nc.vector.tensor_tensor(hid[h][:, :, 2 * u : 2 * u + 2], val[u][:, :, cols].rearrange("p e o -> p o e"),
+                                    gate[u][:, :, cols].rearrange("p e o -> p o e"), ALU.mult)
+
+        codes = [sb.tile([P, HALF], U32, name="codes%d" % h, align_bytes=64) for h in range(2)]
+        hs = [sb.tile([P, HALF], U8, name="hs%d" % h, align_bytes=64) for h in range(2)]
+        gate_pair(0, 0)
+        gate_pair(0, 1)
+        p_sb = {}
+        for h in range(2):
+            gate_pair(1, h)
+            nc.vector.quantize_mx(out=codes[h][:].bitcast(E5M2X4), scales=hs[h][:],
+                                  in_=hid[h][:].rearrange("p o t -> p (o t)"))
+            for m in range(2):
+                acc = ps.tile([P, HALF], F32, name="res%d%d" % (m, h), tag="bank%d" % (2 * h + m))
+                nc.tensor.matmul_mx(out=acc[:], lhsT=bw[:, 2 * P * m : 2 * P * (m + 1)].bitcast(E2M1X4),
+                                    lhsT_scale=bs[:, P * m : P * (m + 1)],
+                                    rhs=codes[h][:].bitcast(E5M2X4), rhs_scale=hs[h][:], start=True, stop=True)
+                p_t = sb.tile([P, HALF], F32, name="p%d%d" % (m, h))
+                nc.scalar.copy(p_t[:], acc[:])
+                p_sb[m, h] = p_t
+
+        def put(on_scalar, page, lst, m, h):
+            window = page[m][:].indirect(lst[:, halves[h][1]])
+            if on_scalar:
+                nc.scalar.activation(out=window, in_=p_sb[m, h][:], func=ACT.Copy)
+            else:
+                nc.vector.tensor_copy(window, p_sb[m, h][:])
+
+        def finish(m, pieces):
+            w = E // pieces
+            for i in range(pieces):
+                y = sb.tile([P, w], F32, name="y%d%d" % (m, i))
+                nc.vector.tensor_tensor(y[:], pa[m][:, i * w : (i + 1) * w], pb[m][:, i * w : (i + 1) * w], ALU.add)
+                nc.sync.dma_start(out=out[P * m : P * (m + 1), i * w : (i + 1) * w], in_=y[:])
+
+        for m in range(2):
+            for h in range(2):
+                put(True, pb, l7, m, h)
+                put(False, pa, l6, m, h)
+            if m == 0:
+                finish(0, 1)
+        finish(1, 2)

@@ -42,13 +42,15 @@ def tile_list_gatedgroupboard_chosen_one_pagetwice_kernel(
             nc.sync.dma_start(t[:], src)
             return t
 
-        xs = late.tile([P, T], U8, name="xs", align_bytes=64, offset=4 * E - T // 2)
+        xs = late.tile([P, T], U8, name="xs", align_bytes=64, offset=16 * J + 4 * E - T // 2)
         ws = sb.tile([P, V], U8, name="ws", align_bytes=64)
         bs = sb.tile([P, N], U8, name="bs", align_bytes=64)
         nc.vector.memset(ws[:].bitcast(I32), 0)
         nc.vector.memset(xs[:].bitcast(I32), 0)
-        nc.vector.memset(bs[:].bitcast(I32), 0)
 
+        warm = sb.tile([P, 2], F32, name="warm")
+        nc.vector.memset(warm[:, 0:1], 0.0)
+        nc.scalar.activation(out=warm[:, 1:2], in_=warm[:, 0:1], func=ACT.Sigmoid)
         l2 = list_tile("l2", offs2)
         xw = sb.tile([P, T], U16, name="xw", align_bytes=64)
         nc.sync.dma_start(out=xw[:].bitcast(I32), in_=xt_words[0].bitcast(I32))
@@ -59,29 +61,26 @@ def tile_list_gatedgroupboard_chosen_one_pagetwice_kernel(
         load_scales(nc.sync, xs, xt_scales)
         l3 = list_tile("l3", offs3)
         l5 = list_tile("l5", offs5)
+        l4 = list_tile("l4", offs4)
 
         def row_values(name, src):
             t = sb.tile([P, PACK], F32, name=name)
             nc.sync.dma_start(out=t[:], in_=src.rearrange("(p t) one -> p (t one)", t=PACK))
             return t
 
+        sa_t = row_values("sa_t", sa)
         sg_t = row_values("sg_t", sg)
         bg_t = row_values("bg_t", bg)
-        l4 = list_tile("l4", offs4)
-        sa_t = row_values("sa_t", sa)
         bw = sb.tile([P, 2 * N], U8, name="bw", align_bytes=64)
         nc.sync.dma_start(out=bw[:].bitcast(I32), in_=wb_words[0].bitcast(I32))
+
+        board = [sb.tile([P, C], F32, name="board%d" % t) for t in range(PACK)]
+        for t in range(PACK):
+            nc.vector.memset(board[t][:], 0.0)
+        nc.vector.memset(bs[:].bitcast(I32), 0)
         load_scales(nc.sync, bs, wb_scales)
         l6 = list_tile("l6", offs6)
         l7 = list_tile("l7", offs7)
-
-        board = [sb.tile([P, C], F32, name="board%d" % t) for t in range(PACK)]
-        pa = [sb.tile([P, E], F32, name="pa0")]
-        pb = [sb.tile([P, E], F32, name="pb0")]
-        for t in range(PACK):
-            nc.vector.memset(board[t][:], 0.0)
-        nc.vector.memset(pa[0][:], 0.0)
-        nc.vector.memset(pb[0][:], 0.0)
 
         xg = sb.tile([P, J], U16, name="xg", align_bytes=64)
         xgs = sb.tile([P, J], U8, name="xgs", align_bytes=64)
@@ -94,43 +93,51 @@ def tile_list_gatedgroupboard_chosen_one_pagetwice_kernel(
         whole = [(slice(0, O), slice(0, O // 16))]
         for cols, lcols in halves:
             nc.vector.tensor_copy(xgs[:, cols], xs[:].indirect(l2[:, lcols]))
-        pa.append(late.tile([P, E], F32, name="pa1", offset=0))
-        pb.append(late.tile([P, E], F32, name="pb1", offset=4 * E))
-        nc.vector.memset(pa[1][:], 0.0)
-        nc.vector.memset(pb[1][:], 0.0)
 
-        a_sb = {}
-        for t in range(PACK):
-            for i, (cols, lcols) in enumerate(halves if t == 0 else whole):
-                w = cols.stop - cols.start
-                acc = ps.tile([P, w], F32, name="acc%d%d" % (t, i), tag="bank%d" % (len(a_sb)))
-                nc.tensor.matmul_mx(out=acc[:], lhsT=wg[:, t, :].bitcast(E4M3X4), lhsT_scale=wgs[:, t, :],
-                                    rhs=xg[:, cols].bitcast(E2M1X4), rhs_scale=xgs[:, cols], start=True, stop=True)
-                a_t = sb.tile([P, w], F32, name="a%d%d" % (t, i))
-                nc.scalar.copy(a_t[:], acc[:])
-                a_sb[t, i] = a_t
+        pa = [late.tile([P, E], F32, name="pa0", offset=16 * J)]
+        pb = [late.tile([P, E], F32, name="pb0", offset=16 * J + 4 * E)]
+        nc.vector.memset(pb[0][:], 0.0)
+        nc.vector.memset(pa[0][:], 0.0)
 
-        val = [sb.tile([P, 2, O], F32, name="val%d" % u) for u in range(2)]
-        gate = [sb.tile([P, 2, O], F32, name="gate%d" % u) for u in range(2)]
-        hid = [sb.tile([P, HALF, PACK], BF16, name="hid%d" % h, align_bytes=64) for h in range(2)]
+        seen = {0: sb.tile([P, 2, 2, O], F32, name="seen0", tag="wg", align_bytes=64)}
+        for h in range(2):
+            seen[1, h] = sb.tile([P, 2, 2, HALF], F32, name="seen1%d" % h, tag="board%d" % (1 - h))
+        hid = [late.tile([P, HALF, PACK], BF16, name="hid%d" % h, align_bytes=64, offset=h * 4 * J) for h in range(2)]
 
-        def fetch(t, cols, lcols):
-            u, e = divmod(t, 2)
-            nc.scalar.activation(out=gate[u][:, e, cols], in_=board[t][:].indirect(l5[:, lcols]), func=ACT.Sigmoid,
+        def fetch(t, key, lcols):
+            nc.scalar.activation(out=seen[key][:, 0, t % 2, :], in_=board[t][:].indirect(l5[:, lcols]), func=ACT.Sigmoid,
                                  bias=bg_t[:, t : t + 1], scale=sg_t[:, t : t + 1])
-            nc.scalar.activation(out=val[u][:, e, cols], in_=board[t][:].indirect(l4[:, lcols]), func=ACT.Copy,
+            nc.scalar.activation(out=seen[key][:, 1, t % 2, :], in_=board[t][:].indirect(l4[:, lcols]), func=ACT.Copy,
                                  scale=sa_t[:, t : t + 1])
 
-        for t in range(PACK):
-            for i, (cols, lcols) in enumerate(halves if t == 0 else whole):
-                nc.vector.tensor_copy(board[t][:].indirect(l3[:, lcols]), a_sb[t, i][:])
-            for cols, lcols in halves if t == PACK - 1 else whole:
-                fetch(t, cols, lcols)
+        def place(piece, slot, t, cols, lcols):
+            w = cols.stop - cols.start
+            acc = ps.tile([P, w], F32, name="acc%d" % piece, tag="bank%d" % piece)
+            nc.tensor.matmul_mx(out=acc[:], lhsT=wg[:, t, :].bitcast(E4M3X4), lhsT_scale=wgs[:, t, :],
+                                rhs=xg[:, cols].bitcast(E2M1X4), rhs_scale=xgs[:, cols], start=True, stop=True)
+            a_t = late.tile([P, w], F32, name="a%d" % piece, offset=slot, align_bytes=64)
+            nc.scalar.copy(a_t[:], acc[:])
+            nc.vector.tensor_copy(board[t][:].indirect(l3[:, lcols]), a_t[:])
+
+        place(0, 8 * J, 0, *halves[0])
+        place(1, 2 * J, 1, *halves[0])
+        place(2, 12 * J, 0, *halves[1])
+        place(3, 14 * J, 1, *halves[1])
+        place(4, 8 * J, 2, *whole[0])
+        place(5, 2 * J, 3, *whole[0])
+        fetch(0, 0, whole[0][1])
+        fetch(1, 0, whole[0][1])
+        for t in range(2, PACK):
+            for h in range(2):
+                fetch(t, (1, h), halves[h][1])
 
         def gate_pair(u, h):
-            cols = halves[h][0]
-            nc.vector.tensor_tensor(hid[h][:, :, 2 * u : 2 * u + 2], val[u][:, :, cols].rearrange("p e o -> p o e"),
-                                    gate[u][:, :, cols].rearrange("p e o -> p o e"), ALU.mult)
+            if u == 0:
+                v, g = seen[0][:, 1, :, halves[h][0]], seen[0][:, 0, :, halves[h][0]]
+            else:
+                v, g = seen[1, h][:, 1, :, :], seen[1, h][:, 0, :, :]
+            nc.vector.tensor_tensor(hid[h][:, :, 2 * u : 2 * u + 2], v.rearrange("p e o -> p o e"),
+                                    g.rearrange("p e o -> p o e"), ALU.mult)
 
         codes = [sb.tile([P, HALF], U32, name="codes%d" % h, align_bytes=64) for h in range(2)]
         hs = [sb.tile([P, HALF], U8, name="hs%d" % h, align_bytes=64) for h in range(2)]
@@ -150,6 +157,11 @@ def tile_list_gatedgroupboard_chosen_one_pagetwice_kernel(
                 nc.scalar.copy(p_t[:], acc[:])
                 p_sb[m, h] = p_t
 
+        pa.append(late.tile([P, E], F32, name="pa1", offset=0))
+        pb.append(sb.tile([P, E], F32, name="pb1", tag="board0"))
+        nc.vector.memset(pb[1][:], 0.0)
+        nc.vector.memset(pa[1][:], 0.0)
+
         def put(on_scalar, page, lst, m, h):
             window = page[m][:].indirect(lst[:, halves[h][1]])
             if on_scalar:
@@ -157,11 +169,11 @@ def tile_list_gatedgroupboard_chosen_one_pagetwice_kernel(
             else:
                 nc.vector.tensor_copy(window, p_sb[m, h][:])
 
-        def finish(m, pieces):
+        def finish(eng, m, pieces):
             w = E // pieces
             for i in range(pieces):
                 y = sb.tile([P, w], F32, name="y%d%d" % (m, i))
-                nc.vector.tensor_tensor(y[:], pa[m][:, i * w : (i + 1) * w], pb[m][:, i * w : (i + 1) * w], ALU.add)
+                eng.tensor_tensor(y[:], pa[m][:, i * w : (i + 1) * w], pb[m][:, i * w : (i + 1) * w], ALU.add)
                 nc.sync.dma_start(out=out[P * m : P * (m + 1), i * w : (i + 1) * w], in_=y[:])
 
         for m in range(2):
@@ -169,5 +181,5 @@ def tile_list_gatedgroupboard_chosen_one_pagetwice_kernel(
                 put(True, pb, l7, m, h)
                 put(False, pa, l6, m, h)
             if m == 0:
-                finish(0, 1)
-        finish(1, 2)
+                finish(nc.vector, 0, 1)
+        finish(nc.vector, 1, 2)

from contextlib import ExitStack

import concourse.mybir as mybir

K, T, J, R, V, C, O, N, E = 512, 1024, 256, 512, 1024, 512, 256, 256, 512
FLOPS = 2 * K * R * J + 2 * R * N * O

F32 = mybir.dt.float32
BF16 = mybir.dt.bfloat16
I32 = mybir.dt.int32
U32 = mybir.dt.uint32
U16 = mybir.dt.uint16
U8 = mybir.dt.uint8
E4M3X4 = mybir.dt.float8_e4m3fn_x4
E5M2X4 = mybir.dt.float8_e5m2_x4
E2M1X4 = mybir.dt.float4_e2m1fn_x4
ACT = mybir.ActivationFunctionType
ALU = mybir.AluOpType

P = 128
PACK = 4
HALF = O // 2


def load_scales(queue, plane, scales):
    for q in range(4):
        queue.dma_start(out=plane[32 * q : 32 * q + 4, :].bitcast(I32), in_=scales[0, 4 * q : 4 * q + 4, :].bitcast(I32))


def tile_list_gatedgroupboard_chosen_one_pagetwice_kernel(
    tc, xt_words, xt_scales, wt_words, wt_scales, sa, sg, bg, wb_words, wb_scales,
    offs, offs2, offs3, offs4, offs5, offs6, offs7, out,
):
    nc = tc.nc
    with ExitStack() as ctx:
        sb = ctx.enter_context(tc.tile_pool(name="sb", bufs=1))
        late = ctx.enter_context(tc.tile_pool(name="late", bufs=1))
        ps = ctx.enter_context(tc.psum_pool(name="ps", bufs=1))

        def list_tile(name, src):
            t = sb.tile([P, src.shape[1]], U16, name=name)
            nc.sync.dma_start(t[:], src)
            return t

        xs = late.tile([P, T], U8, name="xs", align_bytes=64, offset=16 * J + 4 * E - T // 2)
        ws = sb.tile([P, V], U8, name="ws", align_bytes=64)
        bs = sb.tile([P, N], U8, name="bs", align_bytes=64)
        nc.vector.memset(ws[:].bitcast(I32), 0)
        nc.vector.memset(xs[:].bitcast(I32), 0)

        warm = sb.tile([P, 2], F32, name="warm")
        nc.vector.memset(warm[:, 0:1], 0.0)
        nc.scalar.activation(out=warm[:, 1:2], in_=warm[:, 0:1], func=ACT.Sigmoid)
        l2 = list_tile("l2", offs2)
        xw = sb.tile([P, T], U16, name="xw", align_bytes=64)
        nc.sync.dma_start(out=xw[:].bitcast(I32), in_=xt_words[0].bitcast(I32))
        l1 = list_tile("l1", offs)
        load_scales(nc.sync, ws, wt_scales)
        ww = sb.tile([P, V], U32, name="ww", align_bytes=64)
        nc.sync.dma_start(out=ww[:].bitcast(I32), in_=wt_words[0].rearrange("p n t -> p (n t)").bitcast(I32))
        load_scales(nc.sync, xs, xt_scales)
        l3 = list_tile("l3", offs3)
        l5 = list_tile("l5", offs5)
        l4 = list_tile("l4", offs4)

        def row_values(name, src):
            t = sb.tile([P, PACK], F32, name=name)
            nc.sync.dma_start(out=t[:], in_=src.rearrange("(p t) one -> p (t one)", t=PACK))
            return t

        sa_t = row_values("sa_t", sa)
        sg_t = row_values("sg_t", sg)
        bg_t = row_values("bg_t", bg)
        bw = sb.tile([P, 2 * N], U8, name="bw", align_bytes=64)
        nc.sync.dma_start(out=bw[:].bitcast(I32), in_=wb_words[0].bitcast(I32))

        board = [sb.tile([P, C], F32, name="board%d" % t) for t in range(PACK)]
        for t in range(PACK):
            nc.vector.memset(board[t][:], 0.0)
        nc.vector.memset(bs[:].bitcast(I32), 0)
        load_scales(nc.sync, bs, wb_scales)
        l6 = list_tile("l6", offs6)
        l7 = list_tile("l7", offs7)

        xg = sb.tile([P, J], U16, name="xg", align_bytes=64)
        xgs = sb.tile([P, J], U8, name="xgs", align_bytes=64)
        wg = sb.tile([P, PACK, P], U32, name="wg", align_bytes=64)
        wgs = sb.tile([P, PACK, P], U8, name="wgs", align_bytes=64)
        nc.vector.tensor_copy(xg[:], xw[:].indirect(l2[:]))
        nc.vector.tensor_copy(wgs[:].rearrange("p t q -> p q t"), ws[:].indirect(l1[:]))
        nc.vector.tensor_copy(wg[:].rearrange("p t q -> p q t"), ww[:].indirect(l1[:]))
        halves = [(slice(h * HALF, (h + 1) * HALF), slice(h * HALF // 16, (h + 1) * HALF // 16)) for h in range(2)]
        whole = [(slice(0, O), slice(0, O // 16))]
        for cols, lcols in halves:
            nc.vector.tensor_copy(xgs[:, cols], xs[:].indirect(l2[:, lcols]))

        pa = [late.tile([P, E], F32, name="pa0", offset=16 * J)]
        pb = [late.tile([P, E], F32, name="pb0", offset=16 * J + 4 * E)]
        nc.vector.memset(pb[0][:], 0.0)
        nc.vector.memset(pa[0][:], 0.0)

        seen = {0: sb.tile([P, 2, 2, O], F32, name="seen0", tag="wg", align_bytes=64)}
        for h in range(2):
            seen[1, h] = sb.tile([P, 2, 2, HALF], F32, name="seen1%d" % h, tag="board%d" % (1 - h))
        hid = [late.tile([P, HALF, PACK], BF16, name="hid%d" % h, align_bytes=64, offset=h * 4 * J) for h in range(2)]

        def fetch(t, key, lcols):
            nc.scalar.activation(out=seen[key][:, 0, t % 2, :], in_=board[t][:].indirect(l5[:, lcols]), func=ACT.Sigmoid,
                                 bias=bg_t[:, t : t + 1], scale=sg_t[:, t : t + 1])
            nc.scalar.activation(out=seen[key][:, 1, t % 2, :], in_=board[t][:].indirect(l4[:, lcols]), func=ACT.Copy,
                                 scale=sa_t[:, t : t + 1])

        def place(piece, slot, t, cols, lcols):
            w = cols.stop - cols.start
            acc = ps.tile([P, w], F32, name="acc%d" % piece, tag="bank%d" % piece)
            nc.tensor.matmul_mx(out=acc[:], lhsT=wg[:, t, :].bitcast(E4M3X4), lhsT_scale=wgs[:, t, :],
                                rhs=xg[:, cols].bitcast(E2M1X4), rhs_scale=xgs[:, cols], start=True, stop=True)
            a_t = late.tile([P, w], F32, name="a%d" % piece, offset=slot, align_bytes=64)
            nc.scalar.copy(a_t[:], acc[:])
            nc.vector.tensor_copy(board[t][:].indirect(l3[:, lcols]), a_t[:])

        place(0, 8 * J, 0, *halves[0])
        place(1, 2 * J, 1, *halves[0])
        place(2, 12 * J, 0, *halves[1])
        place(3, 14 * J, 1, *halves[1])
        place(4, 8 * J, 2, *whole[0])
        place(5, 2 * J, 3, *whole[0])
        fetch(0, 0, whole[0][1])
        fetch(1, 0, whole[0][1])
        for t in range(2, PACK):
            for h in range(2):
                fetch(t, (1, h), halves[h][1])

        def gate_pair(u, h):
            if u == 0:
                v, g = seen[0][:, 1, :, halves[h][0]], seen[0][:, 0, :, halves[h][0]]
            else:
                v, g = seen[1, h][:, 1, :, :], seen[1, h][:, 0, :, :]
            nc.vector.tensor_tensor(hid[h][:, :, 2 * u : 2 * u + 2], v.rearrange("p e o -> p o e"),
                                    g.rearrange("p e o -> p o e"), ALU.mult)

        codes = [sb.tile([P, HALF], U32, name="codes%d" % h, align_bytes=64) for h in range(2)]
        hs = [sb.tile([P, HALF], U8, name="hs%d" % h, align_bytes=64) for h in range(2)]
        gate_pair(0, 0)
        gate_pair(0, 1)
        p_sb = {}
        for h in range(2):
            gate_pair(1, h)
            nc.vector.quantize_mx(out=codes[h][:].bitcast(E5M2X4), scales=hs[h][:],
                                  in_=hid[h][:].rearrange("p o t -> p (o t)"))
            for m in range(2):
                acc = ps.tile([P, HALF], F32, name="res%d%d" % (m, h), tag="bank%d" % (2 * h + m))
                nc.tensor.matmul_mx(out=acc[:], lhsT=bw[:, 2 * P * m : 2 * P * (m + 1)].bitcast(E2M1X4),
                                    lhsT_scale=bs[:, P * m : P * (m + 1)],
                                    rhs=codes[h][:].bitcast(E5M2X4), rhs_scale=hs[h][:], start=True, stop=True)
                p_t = sb.tile([P, HALF], F32, name="p%d%d" % (m, h))
                nc.scalar.copy(p_t[:], acc[:])
                p_sb[m, h] = p_t

        pa.append(late.tile([P, E], F32, name="pa1", offset=0))
        pb.append(sb.tile([P, E], F32, name="pb1", tag="board0"))
        nc.vector.memset(pb[1][:], 0.0)
        nc.vector.memset(pa[1][:], 0.0)

        def put(on_scalar, page, lst, m, h):
            window = page[m][:].indirect(lst[:, halves[h][1]])
            if on_scalar:
                nc.scalar.activation(out=window, in_=p_sb[m, h][:], func=ACT.Copy)
            else:
                nc.vector.tensor_copy(window, p_sb[m, h][:])

        def finish(eng, m, pieces):
            w = E // pieces
            for i in range(pieces):
                y = sb.tile([P, w], F32, name="y%d%d" % (m, i))
                eng.tensor_tensor(y[:], pa[m][:, i * w : (i + 1) * w], pb[m][:, i * w : (i + 1) * w], ALU.add)
                nc.sync.dma_start(out=out[P * m : P * (m + 1), i * w : (i + 1) * w], in_=y[:])

        for m in range(2):
            for h in range(2):
                put(True, pb, l7, m, h)
                put(False, pa, l6, m, h)
            if m == 0:
                finish(nc.vector, 0, 1)
        finish(nc.vector, 1, 2)
